import numpy as np
import ml_dtypes


def mxq(x, axis, fmt="e4m3"):
    dtype, down = {"e4m3": (ml_dtypes.float8_e4m3fn, 7), "e5m2": (ml_dtypes.float8_e5m2, 14)}[fmt]
    v = np.moveaxis(np.asarray(x, np.float32).astype(ml_dtypes.bfloat16).astype(np.float64), axis, -1)
    blocks = v.reshape(v.shape[:-1] + (-1, 32))
    amax = np.abs(blocks).max(-1, keepdims=True)
    byte = np.maximum(np.where(amax > 0, np.frexp(amax)[1] - 1 + 127, 0) - down, 1)
    scale = np.exp2(byte - 127.0)
    codes = (blocks / scale).astype(np.float32).astype(dtype).astype(np.float64)
    return np.moveaxis((codes * scale).reshape(v.shape), -1, axis)


WIDE = False


def mx_kscale(k):
    if not WIDE:
        return np.ones(k)
    levels = np.array([10, -10, 5, -5, 0])
    if k % 512:
        return np.exp2(np.random.permutation(np.resize(levels, k // 32))).repeat(32)
    a = np.empty((k // 512, 16))
    for p in range(k // 512):
        a[p, :8] = np.random.permutation(np.resize(levels, 8))
        for g in range(8):
            far = levels[np.abs(levels - a[p, g]) >= 10]
            a[p, g + 8] = far[np.random.randint(len(far))]
    return np.exp2(a.ravel()).repeat(32)


def f64(x):
    return np.asarray(x).astype(np.float64)


def striped(idx):
    return np.tile(idx.reshape(-1, 16).T, (8, 1)).astype(np.uint16)


def unstriped(offs):
    return offs[:16].T.reshape(-1).astype(np.int64)

def planes(y):
    n, m = y.shape
    v = y.astype(np.float32).astype(ml_dtypes.bfloat16).astype(np.float64).reshape(n // 32, 32, m)
    top = np.abs(v).max(1)
    byte = np.clip(np.where(top > 0, np.frexp(top)[1] - 1 + 127 - 7, 1), 1, 254)
    codes = (v * np.exp2(127.0 - byte)[:, None, :]).reshape(n, m).astype(np.float32).astype(ml_dtypes.float8_e4m3fn).view(np.uint8)
    words = codes.reshape(n // 512, 128, 4, m).transpose(0, 1, 3, 2)
    return np.ascontiguousarray(words), np.ascontiguousarray(byte.astype(np.uint8).reshape(n // 512, 16, m))


K, T, S, N = 512, 1024, 512, 512


def setup_inputs():
    n = np.random.standard_normal
    s = mx_kscale(K)[:, None]
    return {
        "xT": (n((K, T)) * s).astype(np.float32),
        "w1": (n((K, N)) / np.sqrt(2 * K) / s).astype(np.float32),
        "w2": (n((K, N)) / np.sqrt(2 * K) / s).astype(np.float32),
        "offs": striped(np.random.permutation(T)[:S]),
    }


def reference(xT, w1, w2, offs):
    xq = mxq(f64(xT)[:, unstriped(offs)], 0, "e4m3")
    y0 = mxq(f64(w1), 0, "e4m3").T @ xq
    y1 = mxq(f64(w2), 0, "e4m3").T @ xq
    out_0 = y0 + np.pad(y1, ((0, 0), (1, 0)))[:, :S]
    return (out_0,) + planes(out_0)

@@ -1,0 +1,123 @@
+from contextlib import ExitStack
+
+import concourse.mybir as mybir
+
+K, T, S, N = 512, 1024, 512, 512
+FLOPS = 2 * 2 * K * N * S
+
+F32 = mybir.dt.float32
+BF16 = mybir.dt.bfloat16
+U32 = mybir.dt.uint32
+I32 = mybir.dt.int32
+U16 = mybir.dt.uint16
+U8 = mybir.dt.uint8
+FP8X4 = mybir.dt.float8_e4m3fn_x4
+
+P = 128
+PACK = 4
+PH = S // PACK
+HALF = N // 2
+
+
+def tile_picked_listconv_none_lo_kernel(tc, xT, w1, w2, offs, out_0, out_1, out_2):
+    nc = tc.nc
+    with ExitStack() as ctx:
+        sb = ctx.enter_context(tc.tile_pool(name="sb", bufs=1))
+        psum = ctx.enter_context(tc.psum_pool(name="psum", bufs=1))
+
+        offsets = sb.tile([P, S // 16], U16, name="offsets")
+        x_rows = xT.rearrange("(p j) t -> p j t", j=PACK)
+        x_raw = [sb.tile([P, T], F32, name="x_raw%d" % j, align_bytes=64) for j in range(PACK)]
+        nc.sync.dma_start(out=x_raw[0][:], in_=x_rows[:, 0, :])
+        nc.sync.dma_start(offsets[:], offs)
+        for j in range(1, PACK):
+            nc.sync.dma_start(out=x_raw[j][:], in_=x_rows[:, j, :])
+        w_raw = {}
+        for d, w in enumerate((w1, w2)):
+            w_rows = w.rearrange("(p j) c -> p j c", j=PACK)
+            for h in range(2):
+                w_raw[d, h] = sb.tile([P, PACK, HALF], F32, name="w_raw%d%d" % (d, h), align_bytes=64)
+                nc.sync.dma_start(out=w_raw[d, h][:], in_=w_rows[:, :, h * HALF:(h + 1) * HALF])
+
+        x_bf = sb.tile([P, PACK, PH, PACK], BF16, name="x_bf", align_bytes=64)
+        prev_bf = sb.tile([P, PH * PACK], BF16, name="prev_bf", align_bytes=64)
+        x_codes = sb.tile([P, PH + S], U32, name="x_codes", align_bytes=64)
+        x_scales = sb.tile([P, PH + S], U8, name="x_scales", align_bytes=64)
+        picked = sb.tile([P, PACK, S], F32, name="picked", align_bytes=64)
+        w_bf = [sb.tile([P, PACK, P, PACK], BF16, name="w_bf%d" % d, align_bytes=64) for d in range(2)]
+        w_codes = [sb.tile([P, N], U32, name="w_codes%d" % d, align_bytes=64) for d in range(2)]
+        w_scales = [sb.tile([P, N], U8, name="w_scales%d" % d, align_bytes=64) for d in range(2)]
+
+        def cast_w(copy, d, m0, m1):
+            h = m0 // 64
+            src = w_raw[d, h][:, :, PACK * (m0 - 64 * h):PACK * (m1 - 64 * h)]
+            copy(out=w_bf[d][:, :, m0:m1, :].rearrange("p t m j -> p m t j"),
+                 in_=src.rearrange("p j (m t) -> p m t j", t=PACK))
+
+        def quant_w(d, t):
+            nc.vector.quantize_mx(
+                out=w_codes[d][:, t * P:(t + 1) * P].bitcast(FP8X4),
+                scales=w_scales[d][:, t * P:(t + 1) * P],
+                in_=w_bf[d][:, t, :, :].rearrange("p m j -> p (m j)"))
+
+        nc.vector.memset(prev_bf[:, 0:PACK], 0.0)
+        for j in range(PACK):
+            nc.vector.tensor_copy(picked[:, j, :], x_raw[j][:].indirect(offsets[:]))
+        nc.vector.tensor_copy(out=x_bf[:].rearrange("p r c j -> p c r j"),
+                              in_=picked[:].rearrange("p j (c r) -> p c r j", r=PACK))
+        cast_w(nc.scalar.copy, 0, 0, 64)
+        cast_w(nc.scalar.copy, 0, 64, 96)
+        cast_w(nc.vector.tensor_copy, 0, 96, 128)
+        nc.vector.quantize_mx(out=x_codes[:, PH:].bitcast(FP8X4), scales=x_scales[:, PH:],
+                              in_=x_bf[:].rearrange("p r c j -> p (r c j)"))
+        for t in range(PACK):
+            quant_w(0, t)
+        acc = [psum.tile([P, S], F32, name="acc%d" % t) for t in range(PACK)]
+        for t in range(PACK):
+            nc.tensor.matmul_mx(out=acc[t][:], lhsT=w_codes[0][:, t * P:(t + 1) * P].bitcast(FP8X4),
+                                lhsT_scale=w_scales[0][:, t * P:(t + 1) * P],
+                                rhs=x_codes[:, PH:].bitcast(FP8X4), rhs_scale=x_scales[:, PH:],
+                                start=True, stop=False)
+        nc.vector.tensor_copy(out=prev_bf[:, PACK:],
+                              in_=x_bf[:, PACK - 1, 0:PH - 1, :].rearrange("p c j -> p (c j)"))
+        cast_w(nc.scalar.copy, 1, 0, 64)
+        nc.vector.quantize_mx(out=x_codes[:, :PH].bitcast(FP8X4), scales=x_scales[:, :PH], in_=prev_bf[:])
+        cast_w(nc.vector.tensor_copy, 1, 64, 112)
+        cast_w(nc.scalar.copy, 1, 112, 128)
+        for t in range(PACK):
+            quant_w(1, t)
+
+        y = sb.tile([P, PACK, S], F32, name="y", align_bytes=64)
+        out_rows = out_0.rearrange("(p t) s -> p t s", t=PACK)
+        for t in range(PACK):
+            nc.tensor.matmul_mx(out=acc[t][:], lhsT=w_codes[1][:, t * P:(t + 1) * P].bitcast(FP8X4),
+                                lhsT_scale=w_scales[1][:, t * P:(t + 1) * P],
+                                rhs=x_codes[:, :S].bitcast(FP8X4), rhs_scale=x_scales[:, :S],
+                                start=False, stop=True)
+            copy = nc.scalar.copy if t % 2 == 0 else nc.vector.tensor_copy
+            copy(out=y[:, t, :].rearrange("p (c r) -> p c r", r=PACK),
+                 in_=acc[t][:].rearrange("p (r c) -> p c r", r=PACK))
+            nc.sync.dma_start(out=out_rows[:, t, :], in_=y[:, t, :])
+
+        y_bf = sb.tile([P, S, PACK], BF16, name="y_bf", align_bytes=64)
+        y_codes = sb.tile([P, S], U32, name="y_codes", align_bytes=64)
+        y_scales = sb.tile([P, S], U8, name="y_scales", align_bytes=64)
+        words = out_1.rearrange("z l c r -> l (z c r)").bitcast(I32)
+        scale_rows = out_2.rearrange("z q c -> (z q) c").bitcast(I32)
+
+        def cast_y(copy, s0, s1):
+            copy(out=y_bf[:, s0:s1, :], in_=y[:, :, s0:s1].rearrange("p t s -> p s t"))
+
+        def quant_y(s0, s1):
+            nc.vector.quantize_mx(out=y_codes[:, s0:s1].bitcast(FP8X4), scales=y_scales[:, s0:s1],
+                                  in_=y_bf[:, s0:s1, :].rearrange("p s t -> p (s t)"))
+            nc.sync.dma_start(out=words[:, s0:s1], in_=y_codes[:, s0:s1].bitcast(I32))
+
+        cast_y(nc.vector.tensor_copy, 0, 256)
+        cast_y(nc.scalar.copy, 352, 512)
+        cast_y(nc.vector.tensor_copy, 256, 352)
+        quant_y(0, 256)
+        quant_y(256, 512)
+        for q in range(4):
+            queue = nc.scalar if q % 2 == 0 else nc.sync
+            queue.dma_start(out=scale_rows[4 * q:4 * q + 4, :], in_=y_scales[32 * q:32 * q + 4, :].bitcast(I32))

@@ -15,23 +15,27 @@ FP8X4 = mybir.dt.float8_e4m3fn_x4
 
 P = 128
 PACK = 4
-PH = S // PACK
-HALF = N // 2
+HALF = 256
+RUN = HALF // PACK
+SPAN = RUN + HALF
 
 
 def tile_picked_listconv_none_lo_kernel(tc, xT, w1, w2, offs, out_0, out_1, out_2):
     nc = tc.nc
+    vcopy, scopy = nc.vector.tensor_copy, nc.scalar.copy
     with ExitStack() as ctx:
         sb = ctx.enter_context(tc.tile_pool(name="sb", bufs=1))
         psum = ctx.enter_context(tc.psum_pool(name="psum", bufs=1))
 
         offsets = sb.tile([P, S // 16], U16, name="offsets")
         x_rows = xT.rearrange("(p j) t -> p j t", j=PACK)
-        x_raw = [sb.tile([P, T], F32, name="x_raw%d" % j, align_bytes=64) for j in range(PACK)]
-        nc.sync.dma_start(out=x_raw[0][:], in_=x_rows[:, 0, :])
-        nc.sync.dma_start(offsets[:], offs)
-        for j in range(1, PACK):
-            nc.sync.dma_start(out=x_raw[j][:], in_=x_rows[:, j, :])
+        x_raw = {}
+        for u in range(2):
+            for a in range(2):
+                x_raw[u, a] = sb.tile([P, 2, T // 2], F32, name="x_raw%d%d" % (u, a), align_bytes=64)
+                nc.sync.dma_start(out=x_raw[u, a][:], in_=x_rows[:, 2 * u:2 * u + 2, a * T // 2:(a + 1) * T // 2])
+                if (u, a) == (0, 1):
+                    nc.sync.dma_start(offsets[:], offs)
         w_raw = {}
         for d, w in enumerate((w1, w2)):
             w_rows = w.rearrange("(p j) c -> p j c", j=PACK)
@@ -39,18 +43,40 @@ def tile_picked_listconv_none_lo_kernel(tc, xT, w1, w2, offs, out_0, out_1, out_
                 w_raw[d, h] = sb.tile([P, PACK, HALF], F32, name="w_raw%d%d" % (d, h), align_bytes=64)
                 nc.sync.dma_start(out=w_raw[d, h][:], in_=w_rows[:, :, h * HALF:(h + 1) * HALF])
 
-        x_bf = sb.tile([P, PACK, PH, PACK], BF16, name="x_bf", align_bytes=64)
-        prev_bf = sb.tile([P, PH * PACK], BF16, name="prev_bf", align_bytes=64)
-        x_codes = sb.tile([P, PH + S], U32, name="x_codes", align_bytes=64)
-        x_scales = sb.tile([P, PH + S], U8, name="x_scales", align_bytes=64)
-        picked = sb.tile([P, PACK, S], F32, name="picked", align_bytes=64)
+        pairs = [sb.tile([P, T], U32, name="pairs%d" % u, align_bytes=64) for u in range(2)]
+        picked = sb.tile([P, 2, PACK + S], U32, name="picked", align_bytes=64)
+        x_codes = [sb.tile([P, SPAN], U32, name="x_codes%d" % h, align_bytes=64) for h in range(2)]
+        x_scales = [sb.tile([P, SPAN], U8, name="x_scales%d" % h, align_bytes=64) for h in range(2)]
         w_bf = [sb.tile([P, PACK, P, PACK], BF16, name="w_bf%d" % d, align_bytes=64) for d in range(2)]
         w_codes = [sb.tile([P, N], U32, name="w_codes%d" % d, align_bytes=64) for d in range(2)]
         w_scales = [sb.tile([P, N], U8, name="w_scales%d" % d, align_bytes=64) for d in range(2)]
 
+        x_bf0 = sb.tile([P, HALF * PACK], BF16, name="x_bf0", align_bytes=64)
+        reused = w_bf[0][:].rearrange("p t m j -> p (t m j)")
+        x_bf = [x_bf0[:], reused[:, :HALF * PACK]]
+        prev_bf = reused[:, HALF * PACK:HALF * PACK + 2 * RUN * PACK]
+
+        def cast_x(copy, u, t0, t1):
+            a = t0 // (T // 2)
+            src = x_raw[u, a][:, :, t0 - a * T // 2:t1 - a * T // 2]
+            copy(out=pairs[u][:, t0:t1].bitcast(BF16).rearrange("p (t j) -> p t j", j=2),
+                 in_=src.rearrange("p j t -> p t j"))
+
+        def gather(u):
+            vcopy(picked[:, u, PACK:], pairs[u][:].indirect(offsets[:]))
+
+        def weave(copy, dt, h):
+            src = picked[:, :, PACK + h * HALF:PACK + (h + 1) * HALF].bitcast(dt)
+            copy(out=x_bf[h].bitcast(dt).rearrange("p (r c u) -> p c r u", r=PACK, u=2),
+                 in_=src.rearrange("p u (c r) -> p c r u", r=PACK))
+
+        def quant_x(h):
+            nc.vector.quantize_mx(out=x_codes[h][:, RUN:].bitcast(FP8X4), scales=x_scales[h][:, RUN:],
+                                  in_=x_bf[h])
+
         def cast_w(copy, d, m0, m1):
-            h = m0 // 64
-            src = w_raw[d, h][:, :, PACK * (m0 - 64 * h):PACK * (m1 - 64 * h)]
+            h = m0 // RUN
+            src = w_raw[d, h][:, :, PACK * (m0 - RUN * h):PACK * (m1 - RUN * h)]
             copy(out=w_bf[d][:, :, m0:m1, :].rearrange("p t m j -> p m t j"),
                  in_=src.rearrange("p j (m t) -> p m t j", t=PACK))
 
@@ -60,64 +86,82 @@ def tile_picked_listconv_none_lo_kernel(tc, xT, w1, w2, offs, out_0, out_1, out_
                 scales=w_scales[d][:, t * P:(t + 1) * P],
                 in_=w_bf[d][:, t, :, :].rearrange("p m j -> p (m j)"))
 
-        nc.vector.memset(prev_bf[:, 0:PACK], 0.0)
-        for j in range(PACK):
-            nc.vector.tensor_copy(picked[:, j, :], x_raw[j][:].indirect(offsets[:]))
-        nc.vector.tensor_copy(out=x_bf[:].rearrange("p r c j -> p c r j"),
-                              in_=picked[:].rearrange("p j (c r) -> p c r j", r=PACK))
-        cast_w(nc.scalar.copy, 0, 0, 64)
-        cast_w(nc.scalar.copy, 0, 64, 96)
-        cast_w(nc.vector.tensor_copy, 0, 96, 128)
-        nc.vector.quantize_mx(out=x_codes[:, PH:].bitcast(FP8X4), scales=x_scales[:, PH:],
-                              in_=x_bf[:].rearrange("p r c j -> p (r c j)"))
+        acc = {(h, t): psum.tile([P, HALF], F32, name="acc%d%d" % (h, t)) for h in range(2) for t in range(PACK)}
+
+        def tap(d, h, t):
+            c0 = RUN * (1 - d)
+            nc.tensor.matmul_mx(out=acc[h, t][:], lhsT=w_codes[d][:, t * P:(t + 1) * P].bitcast(FP8X4),
+                                lhsT_scale=w_scales[d][:, t * P:(t + 1) * P],
+                                rhs=x_codes[h][:, c0:c0 + HALF].bitcast(FP8X4),
+                                rhs_scale=x_scales[h][:, c0:c0 + HALF],
+                                start=(d == 0), stop=(d == 1))
+
+        nc.vector.memset(picked[:, :, 0:PACK], 0)
+        cast_x(vcopy, 0, 0, 512)
+        cast_x(vcopy, 0, 512, 1024)
+        gather(0)
+        cast_x(scopy, 1, 0, 512)
+        cast_x(vcopy, 1, 512, 848)
+        cast_x(scopy, 1, 848, 1024)
+        gather(1)
+        weave(vcopy, I32, 0)
+        cast_w(scopy, 0, 0, 64)
+        cast_w(vcopy, 0, 64, 92)
+        cast_w(scopy, 0, 92, 128)
+        quant_x(0)
         for t in range(PACK):
             quant_w(0, t)
-        acc = [psum.tile([P, S], F32, name="acc%d" % t) for t in range(PACK)]
         for t in range(PACK):
-            nc.tensor.matmul_mx(out=acc[t][:], lhsT=w_codes[0][:, t * P:(t + 1) * P].bitcast(FP8X4),
-                                lhsT_scale=w_scales[0][:, t * P:(t + 1) * P],
-                                rhs=x_codes[:, PH:].bitcast(FP8X4), rhs_scale=x_scales[:, PH:],
-                                start=True, stop=False)
-        nc.vector.tensor_copy(out=prev_bf[:, PACK:],
-                              in_=x_bf[:, PACK - 1, 0:PH - 1, :].rearrange("p c j -> p (c j)"))
-        cast_w(nc.scalar.copy, 1, 0, 64)
-        nc.vector.quantize_mx(out=x_codes[:, :PH].bitcast(FP8X4), scales=x_scales[:, :PH], in_=prev_bf[:])
-        cast_w(nc.vector.tensor_copy, 1, 64, 112)
-        cast_w(nc.scalar.copy, 1, 112, 128)
+            tap(0, 0, t)
+        weave(vcopy, I32, 1)
+        vcopy(out=prev_bf.bitcast(I32).rearrange("p (c u) -> p c u", u=2),
+              in_=picked[:, :, PACK - 1:PACK - 1 + S:PACK].bitcast(I32).rearrange("p u c -> p c u"))
+        quant_x(1)
+        cast_w(scopy, 1, 0, 64)
+        for h in range(2):
+            nc.vector.quantize_mx(out=x_codes[h][:, :RUN].bitcast(FP8X4), scales=x_scales[h][:, :RUN],
+                                  in_=prev_bf[:, h * HALF:(h + 1) * HALF])
+        cast_w(vcopy, 1, 64, 84)
+        cast_w(scopy, 1, 84, 128)
         for t in range(PACK):
             quant_w(1, t)
 
-        y = sb.tile([P, PACK, S], F32, name="y", align_bytes=64)
-        out_rows = out_0.rearrange("(p t) s -> p t s", t=PACK)
-        for t in range(PACK):
-            nc.tensor.matmul_mx(out=acc[t][:], lhsT=w_codes[1][:, t * P:(t + 1) * P].bitcast(FP8X4),
-                                lhsT_scale=w_scales[1][:, t * P:(t + 1) * P],
-                                rhs=x_codes[:, :S].bitcast(FP8X4), rhs_scale=x_scales[:, :S],
-                                start=False, stop=True)
-            copy = nc.scalar.copy if t % 2 == 0 else nc.vector.tensor_copy
-            copy(out=y[:, t, :].rearrange("p (c r) -> p c r", r=PACK),
-                 in_=acc[t][:].rearrange("p (r c) -> p c r", r=PACK))
-            nc.sync.dma_start(out=out_rows[:, t, :], in_=y[:, t, :])
-
+        y = [sb.tile([P, PACK, HALF], F32, name="y%d" % h, align_bytes=64) for h in range(2)]
         y_bf = sb.tile([P, S, PACK], BF16, name="y_bf", align_bytes=64)
         y_codes = sb.tile([P, S], U32, name="y_codes", align_bytes=64)
         y_scales = sb.tile([P, S], U8, name="y_scales", align_bytes=64)
+        out_rows = out_0.rearrange("(p t) s -> p t s", t=PACK)
         words = out_1.rearrange("z l c r -> l (z c r)").bitcast(I32)
         scale_rows = out_2.rearrange("z q c -> (z q) c").bitcast(I32)
 
         def cast_y(copy, s0, s1):
-            copy(out=y_bf[:, s0:s1, :], in_=y[:, :, s0:s1].rearrange("p t s -> p s t"))
+            h = s0 // HALF
+            copy(out=y_bf[:, s0:s1, :], in_=y[h][:, :, s0 - h * HALF:s1 - h * HALF].rearrange("p t s -> p s t"))
 
         def quant_y(s0, s1):
             nc.vector.quantize_mx(out=y_codes[:, s0:s1].bitcast(FP8X4), scales=y_scales[:, s0:s1],
                                   in_=y_bf[:, s0:s1, :].rearrange("p s t -> p (s t)"))
             nc.sync.dma_start(out=words[:, s0:s1], in_=y_codes[:, s0:s1].bitcast(I32))
 
-        cast_y(nc.vector.tensor_copy, 0, 256)
-        cast_y(nc.scalar.copy, 352, 512)
-        cast_y(nc.vector.tensor_copy, 256, 352)
-        quant_y(0, 256)
-        quant_y(256, 512)
+        evac = "svsvsssv"
+        for h in range(2):
+            if h == 1:
+                for t in range(PACK):
+                    tap(0, 1, t)
+            for t in range(PACK):
+                tap(1, h, t)
+                copy = scopy if evac[PACK * h + t] == "s" else vcopy
+                copy(out=y[h][:, t, :].rearrange("p (c r) -> p c r", r=PACK),
+                     in_=acc[h, t][:].rearrange("p (r c) -> p c r", r=PACK))
+                t0 = {(0, 0): 0, (0, 1): 1, (0, 3): 2, (1, 1): 0, (1, 3): 2}.get((h, t))
+                if t0 is not None:
+                    nc.sync.dma_start(out=out_rows[:, t0:t + 1, h * HALF:(h + 1) * HALF], in_=y[h][:, t0:t + 1, :])
+            if h == 0:
+                cast_y(vcopy, 0, HALF)
+        quant_y(0, HALF)
+        cast_y(vcopy, HALF, 416)
+        cast_y(scopy, 416, S)
+        quant_y(HALF, S)
         for q in range(4):
             queue = nc.scalar if q % 2 == 0 else nc.sync
             queue.dma_start(out=scale_rows[4 * q:4 * q + 4, :], in_=y_scales[32 * q:32 * q + 4, :].bitcast(I32))

@@ -28,57 +28,34 @@ def tile_picked_listconv_none_lo_kernel(tc, xT, w1, w2, offs, out_0, out_1, out_
         psum = ctx.enter_context(tc.psum_pool(name="psum", bufs=1))
 
         offsets = sb.tile([P, S // 16], U16, name="offsets")
+        nc.sync.dma_start(offsets[:], offs)
         x_rows = xT.rearrange("(p j) t -> p j t", j=PACK)
-        x_raw = {}
-        for u in range(2):
-            for a in range(2):
-                x_raw[u, a] = sb.tile([P, 2, T // 2], F32, name="x_raw%d%d" % (u, a), align_bytes=64)
-                nc.sync.dma_start(out=x_raw[u, a][:], in_=x_rows[:, 2 * u:2 * u + 2, a * T // 2:(a + 1) * T // 2])
-                if (u, a) == (0, 1):
-                    nc.sync.dma_start(offsets[:], offs)
-        w_raw = {}
+        x_raw = [sb.tile([P, T], F32, name="x_raw%d" % j, align_bytes=64) for j in range(PACK)]
+        for j in (0, 2, 1, 3):
+            nc.sync.dma_start(out=x_raw[j][:], in_=x_rows[:, j, :])
+        w_raw = [sb.tile([P, PACK, N], F32, name="w_raw%d" % d, align_bytes=64) for d in range(2)]
         for d, w in enumerate((w1, w2)):
-            w_rows = w.rearrange("(p j) c -> p j c", j=PACK)
-            for h in range(2):
-                w_raw[d, h] = sb.tile([P, PACK, HALF], F32, name="w_raw%d%d" % (d, h), align_bytes=64)
-                nc.sync.dma_start(out=w_raw[d, h][:], in_=w_rows[:, :, h * HALF:(h + 1) * HALF])
+            nc.sync.dma_start(out=w_raw[d][:], in_=w.rearrange("(p j) c -> p j c", j=PACK))
 
-        pairs = [sb.tile([P, T], U32, name="pairs%d" % u, align_bytes=64) for u in range(2)]
-        picked = sb.tile([P, 2, PACK + S], U32, name="picked", align_bytes=64)
+        x_half = [sb.tile([P, T], BF16, name="x_half%d" % j, align_bytes=64) for j in range(2)]
+        x_bf = sb.tile([P, 2, PACK, RUN * PACK], BF16, name="x_bf", align_bytes=64)
         x_codes = [sb.tile([P, SPAN], U32, name="x_codes%d" % h, align_bytes=64) for h in range(2)]
         x_scales = [sb.tile([P, SPAN], U8, name="x_scales%d" % h, align_bytes=64) for h in range(2)]
         w_bf = [sb.tile([P, PACK, P, PACK], BF16, name="w_bf%d" % d, align_bytes=64) for d in range(2)]
         w_codes = [sb.tile([P, N], U32, name="w_codes%d" % d, align_bytes=64) for d in range(2)]
         w_scales = [sb.tile([P, N], U8, name="w_scales%d" % d, align_bytes=64) for d in range(2)]
+        prev_bf = w_bf[0][:, 0, :, :].rearrange("p (h c) j -> p h (c j)", h=2)
 
-        x_bf0 = sb.tile([P, HALF * PACK], BF16, name="x_bf0", align_bytes=64)
-        reused = w_bf[0][:].rearrange("p t m j -> p (t m j)")
-        x_bf = [x_bf0[:], reused[:, :HALF * PACK]]
-        prev_bf = reused[:, HALF * PACK:HALF * PACK + 2 * RUN * PACK]
-
-        def cast_x(copy, u, t0, t1):
-            a = t0 // (T // 2)
-            src = x_raw[u, a][:, :, t0 - a * T // 2:t1 - a * T // 2]
-            copy(out=pairs[u][:, t0:t1].bitcast(BF16).rearrange("p (t j) -> p t j", j=2),
-                 in_=src.rearrange("p j t -> p t j"))
-
-        def gather(u):
-            vcopy(picked[:, u, PACK:], pairs[u][:].indirect(offsets[:]))
-
-        def weave(copy, dt, h):
-            src = picked[:, :, PACK + h * HALF:PACK + (h + 1) * HALF].bitcast(dt)
-            copy(out=x_bf[h].bitcast(dt).rearrange("p (r c u) -> p c r u", r=PACK, u=2),
-                 in_=src.rearrange("p u (c r) -> p c r u", r=PACK))
+        x_slots = x_bf[:].rearrange("p h r (c j) -> p h c r j", j=PACK)
 
         def quant_x(h):
             nc.vector.quantize_mx(out=x_codes[h][:, RUN:].bitcast(FP8X4), scales=x_scales[h][:, RUN:],
-                                  in_=x_bf[h])
+                                  in_=x_bf[:, h, :, :].rearrange("p r n -> p (r n)"))
 
-        def cast_w(copy, d, m0, m1):
-            h = m0 // RUN
-            src = w_raw[d, h][:, :, PACK * (m0 - RUN * h):PACK * (m1 - RUN * h)]
-            copy(out=w_bf[d][:, :, m0:m1, :].rearrange("p t m j -> p m t j"),
-                 in_=src.rearrange("p j (m t) -> p m t j", t=PACK))
+        def cast_w(copy, d, t0, m0, m1):
+            src = w_raw[d][:].rearrange("p j (m t) -> p m j t", t=PACK)
+            copy(out=w_bf[d][:, t0:t0 + 2, m0:m1, :].rearrange("p t m j -> p m j t"),
+                 in_=src[:, m0:m1, :, t0:t0 + 2])
 
         def quant_w(d, t):
             nc.vector.quantize_mx(
@@ -96,37 +73,43 @@ def tile_picked_listconv_none_lo_kernel(tc, xT, w1, w2, offs, out_0, out_1, out_
                                 rhs_scale=x_scales[h][:, c0:c0 + HALF],
                                 start=(d == 0), stop=(d == 1))
 
-        nc.vector.memset(picked[:, :, 0:PACK], 0)
-        cast_x(vcopy, 0, 0, 512)
-        cast_x(vcopy, 0, 512, 1024)
-        gather(0)
-        cast_x(scopy, 1, 0, 512)
-        cast_x(vcopy, 1, 512, 848)
-        cast_x(scopy, 1, 848, 1024)
-        gather(1)
-        weave(vcopy, I32, 0)
-        cast_w(scopy, 0, 0, 64)
-        cast_w(vcopy, 0, 64, 92)
-        cast_w(scopy, 0, 92, 128)
+        copy_func = mybir.ActivationFunctionType.Copy
+        vcopy(out=x_half[0][:], in_=x_raw[0][:])
+        nc.scalar.activation(x_slots[:, :, :, :, 0], x_half[0][:].indirect(offsets[:]), copy_func)
+        vcopy(x_slots[:, :, :, :, 2], x_raw[2][:].indirect(offsets[:]))
+        vcopy(out=x_half[1][:], in_=x_raw[1][:])
+        for h in (1, 0):
+            entries = offsets[:, h * HALF // 16:(h + 1) * HALF // 16]
+            nc.scalar.activation(x_slots[:, h, :, :, 1], x_half[1][:].indirect(entries), copy_func)
+            vcopy(x_slots[:, h, :, :, 3], x_raw[3][:].indirect(entries))
+        quant_x(1)
+        for i in range(4):
+            nc.tensor.matmul_mx(out=acc[i % 2, 1][:], lhsT=x_codes[1][:, RUN:RUN + P].bitcast(FP8X4),
+                                lhsT_scale=x_scales[1][:, RUN:RUN + P],
+                                rhs=x_codes[1][:, RUN:].bitcast(FP8X4), rhs_scale=x_scales[1][:, RUN:],
+                                start=True, stop=True)
         quant_x(0)
+        cast_w(vcopy, 0, 0, 0, P)
+        cast_w(vcopy, 0, 2, 0, 32)
+        cast_w(scopy, 0, 2, 32, P)
         for t in range(PACK):
             quant_w(0, t)
-        for t in range(PACK):
-            tap(0, 0, t)
-        weave(vcopy, I32, 1)
-        vcopy(out=prev_bf.bitcast(I32).rearrange("p (c u) -> p c u", u=2),
-              in_=picked[:, :, PACK - 1:PACK - 1 + S:PACK].bitcast(I32).rearrange("p u c -> p c u"))
-        quant_x(1)
-        cast_w(scopy, 1, 0, 64)
+            for h in range(2):
+                tap(0, h, t)
+        nc.vector.memset(prev_bf[:, 0, 0:PACK], 0.0)
+        vcopy(out=prev_bf[:, :, PACK:], in_=x_bf[:, :, PACK - 1, :HALF - PACK])
+        vcopy(out=prev_bf[:, 1, :PACK], in_=x_bf[:, 0, PACK - 1, HALF - PACK:])
+        cast_w(vcopy, 1, 0, 0, 88)
+        cast_w(scopy, 1, 0, 88, P)
         for h in range(2):
             nc.vector.quantize_mx(out=x_codes[h][:, :RUN].bitcast(FP8X4), scales=x_scales[h][:, :RUN],
-                                  in_=prev_bf[:, h * HALF:(h + 1) * HALF])
-        cast_w(vcopy, 1, 64, 84)
-        cast_w(scopy, 1, 84, 128)
+                                  in_=prev_bf[:, h, :])
+        cast_w(vcopy, 1, 2, 0, 56)
+        cast_w(scopy, 1, 2, 56, P)
         for t in range(PACK):
             quant_w(1, t)
 
-        y = [sb.tile([P, PACK, HALF], F32, name="y%d" % h, align_bytes=64) for h in range(2)]
+        y = sb.tile([P, PACK, S], F32, name="y", align_bytes=64)
         y_bf = sb.tile([P, S, PACK], BF16, name="y_bf", align_bytes=64)
         y_codes = sb.tile([P, S], U32, name="y_codes", align_bytes=64)
         y_scales = sb.tile([P, S], U8, name="y_scales", align_bytes=64)
@@ -134,33 +117,33 @@ def tile_picked_listconv_none_lo_kernel(tc, xT, w1, w2, offs, out_0, out_1, out_
         words = out_1.rearrange("z l c r -> l (z c r)").bitcast(I32)
         scale_rows = out_2.rearrange("z q c -> (z q) c").bitcast(I32)
 
+        def finish(copy, h, t):
+            tap(1, h, t)
+            copy(out=y[:, t, h * HALF:(h + 1) * HALF].rearrange("p (c r) -> p c r", r=PACK),
+                 in_=acc[h, t][:].rearrange("p (r c) -> p c r", r=PACK))
+
         def cast_y(copy, s0, s1):
-            h = s0 // HALF
-            copy(out=y_bf[:, s0:s1, :], in_=y[h][:, :, s0 - h * HALF:s1 - h * HALF].rearrange("p t s -> p s t"))
+            copy(out=y_bf[:, s0:s1, :].rearrange("p (c i) t -> p c t i", i=PACK),
+                 in_=y[:, :, s0:s1].rearrange("p t (c i) -> p c t i", i=PACK))
 
         def quant_y(s0, s1):
             nc.vector.quantize_mx(out=y_codes[:, s0:s1].bitcast(FP8X4), scales=y_scales[:, s0:s1],
                                   in_=y_bf[:, s0:s1, :].rearrange("p s t -> p (s t)"))
             nc.sync.dma_start(out=words[:, s0:s1], in_=y_codes[:, s0:s1].bitcast(I32))
 
-        evac = "svsvsssv"
-        for h in range(2):
-            if h == 1:
-                for t in range(PACK):
-                    tap(0, 1, t)
-            for t in range(PACK):
-                tap(1, h, t)
-                copy = scopy if evac[PACK * h + t] == "s" else vcopy
-                copy(out=y[h][:, t, :].rearrange("p (c r) -> p c r", r=PACK),
-                     in_=acc[h, t][:].rearrange("p (r c) -> p c r", r=PACK))
-                t0 = {(0, 0): 0, (0, 1): 1, (0, 3): 2, (1, 1): 0, (1, 3): 2}.get((h, t))
-                if t0 is not None:
-                    nc.sync.dma_start(out=out_rows[:, t0:t + 1, h * HALF:(h + 1) * HALF], in_=y[h][:, t0:t + 1, :])
-            if h == 0:
-                cast_y(vcopy, 0, HALF)
+        for t in range(2):
+            finish(scopy, 0, t)
+            finish(vcopy, 1, t)
+            nc.sync.dma_start(out=out_rows[:, t, :], in_=y[:, t, :])
+        finish(scopy, 0, 2)
+        finish(vcopy, 0, 3)
+        finish(scopy, 1, 2)
+        finish(scopy, 1, 3)
+        nc.sync.dma_start(out=out_rows[:, 2:, :], in_=y[:, 2:, :])
+        cast_y(vcopy, 0, HALF)
+        cast_y(vcopy, HALF, 384)
+        cast_y(scopy, 384, S)
         quant_y(0, HALF)
-        cast_y(vcopy, HALF, 416)
-        cast_y(scopy, 416, S)
         quant_y(HALF, S)
         for q in range(4):
             queue = nc.scalar if q % 2 == 0 else nc.sync

@@ -28,34 +28,58 @@ def tile_picked_listconv_none_lo_kernel(tc, xT, w1, w2, offs, out_0, out_1, out_
         psum = ctx.enter_context(tc.psum_pool(name="psum", bufs=1))
 
         offsets = sb.tile([P, S // 16], U16, name="offsets")
-        nc.sync.dma_start(offsets[:], offs)
         x_rows = xT.rearrange("(p j) t -> p j t", j=PACK)
         x_raw = [sb.tile([P, T], F32, name="x_raw%d" % j, align_bytes=64) for j in range(PACK)]
+        nc.sync.dma_start(offsets[:], offs)
         for j in (0, 2, 1, 3):
             nc.sync.dma_start(out=x_raw[j][:], in_=x_rows[:, j, :])
         w_raw = [sb.tile([P, PACK, N], F32, name="w_raw%d" % d, align_bytes=64) for d in range(2)]
-        for d, w in enumerate((w1, w2)):
-            nc.sync.dma_start(out=w_raw[d][:], in_=w.rearrange("(p j) c -> p j c", j=PACK))
+        nc.sync.dma_start(out=w_raw[0][:], in_=w1.rearrange("(p j) c -> p j c", j=PACK))
+        for j0 in (0, 2):
+            nc.sync.dma_start(out=w_raw[1][:, j0:j0 + 2, :],
+                              in_=w2.rearrange("(p j) c -> p j c", j=PACK)[:, j0:j0 + 2, :])
 
         x_half = [sb.tile([P, T], BF16, name="x_half%d" % j, align_bytes=64) for j in range(2)]
         x_bf = sb.tile([P, 2, PACK, RUN * PACK], BF16, name="x_bf", align_bytes=64)
-        x_codes = [sb.tile([P, SPAN], U32, name="x_codes%d" % h, align_bytes=64) for h in range(2)]
-        x_scales = [sb.tile([P, SPAN], U8, name="x_scales%d" % h, align_bytes=64) for h in range(2)]
+        front_bf = sb.tile([P, 2, RUN * PACK], BF16, name="front_bf", align_bytes=64)
+        x_codes = sb.tile([P, 2 * SPAN], U32, name="x_codes", align_bytes=64)
+        x_scales = sb.tile([P, 2 * SPAN], U8, name="x_scales", align_bytes=64)
         w_bf = [sb.tile([P, PACK, P, PACK], BF16, name="w_bf%d" % d, align_bytes=64) for d in range(2)]
         w_codes = [sb.tile([P, N], U32, name="w_codes%d" % d, align_bytes=64) for d in range(2)]
         w_scales = [sb.tile([P, N], U8, name="w_scales%d" % d, align_bytes=64) for d in range(2)]
-        prev_bf = w_bf[0][:, 0, :, :].rearrange("p (h c) j -> p h (c j)", h=2)
 
+        copy_func = mybir.ActivationFunctionType.Copy
         x_slots = x_bf[:].rearrange("p h r (c j) -> p h c r j", j=PACK)
 
+        def slots(j, s0, s1):
+            h, c0 = divmod(s0 // PACK, RUN)
+            return x_slots[:, h, c0:c0 + (s1 - s0) // PACK, :, j]
+
+        def vgather(j, s0, s1):
+            vcopy(slots(j, s0, s1), x_raw[j][:].indirect(offsets[:, s0 // 16:s1 // 16]))
+
+        def sgather(j, s0, s1):
+            nc.scalar.activation(slots(j, s0, s1), x_half[j][:].indirect(offsets[:, s0 // 16:s1 // 16]), copy_func)
+
         def quant_x(h):
-            nc.vector.quantize_mx(out=x_codes[h][:, RUN:].bitcast(FP8X4), scales=x_scales[h][:, RUN:],
+            c0 = h * SPAN + RUN
+            nc.vector.quantize_mx(out=x_codes[:, c0:c0 + HALF].bitcast(FP8X4), scales=x_scales[:, c0:c0 + HALF],
                                   in_=x_bf[:, h, :, :].rearrange("p r n -> p (r n)"))
+
+        def quant_front(h):
+            c0 = h * SPAN
+            nc.vector.quantize_mx(out=x_codes[:, c0:c0 + RUN].bitcast(FP8X4), scales=x_scales[:, c0:c0 + RUN],
+                                  in_=front_bf[:, h, :])
 
         def cast_w(copy, d, t0, m0, m1):
             src = w_raw[d][:].rearrange("p j (m t) -> p m j t", t=PACK)
             copy(out=w_bf[d][:, t0:t0 + 2, m0:m1, :].rearrange("p t m j -> p m j t"),
                  in_=src[:, m0:m1, :, t0:t0 + 2])
+
+        def cast_w2_pair(copy, j0, m0, m1):
+            src = w_raw[1][:, j0:j0 + 2, :].rearrange("p j (a i t) -> p a t i j", i=2, t=PACK)
+            dst = w_bf[1][:, :, :, j0:j0 + 2].rearrange("p t (a i) j -> p a t i j", i=2)
+            copy(out=dst[:, m0 // 2:m1 // 2, 0:2], in_=src[:, m0 // 2:m1 // 2, 0:2])
 
         def quant_w(d, t):
             nc.vector.quantize_mx(
@@ -66,47 +90,54 @@ def tile_picked_listconv_none_lo_kernel(tc, xT, w1, w2, offs, out_0, out_1, out_
         acc = {(h, t): psum.tile([P, HALF], F32, name="acc%d%d" % (h, t)) for h in range(2) for t in range(PACK)}
 
         def tap(d, h, t):
-            c0 = RUN * (1 - d)
+            c0 = h * SPAN + RUN * (1 - d)
             nc.tensor.matmul_mx(out=acc[h, t][:], lhsT=w_codes[d][:, t * P:(t + 1) * P].bitcast(FP8X4),
                                 lhsT_scale=w_scales[d][:, t * P:(t + 1) * P],
-                                rhs=x_codes[h][:, c0:c0 + HALF].bitcast(FP8X4),
-                                rhs_scale=x_scales[h][:, c0:c0 + HALF],
+                                rhs=x_codes[:, c0:c0 + HALF].bitcast(FP8X4),
+                                rhs_scale=x_scales[:, c0:c0 + HALF],
                                 start=(d == 0), stop=(d == 1))
 
-        copy_func = mybir.ActivationFunctionType.Copy
+        zeros = sb.tile([P, PACK], BF16, name="zeros")
+        nc.vector.memset(zeros[:], 0.0)
+        nc.scalar.activation(front_bf[:, 0, :PACK], zeros[:], copy_func)
         vcopy(out=x_half[0][:], in_=x_raw[0][:])
-        nc.scalar.activation(x_slots[:, :, :, :, 0], x_half[0][:].indirect(offsets[:]), copy_func)
+        sgather(0, HALF, S)
+        sgather(0, 128, HALF)
+        vgather(0, 0, 128)
         vcopy(x_slots[:, :, :, :, 2], x_raw[2][:].indirect(offsets[:]))
-        vcopy(out=x_half[1][:], in_=x_raw[1][:])
-        for h in (1, 0):
-            entries = offsets[:, h * HALF // 16:(h + 1) * HALF // 16]
-            nc.scalar.activation(x_slots[:, h, :, :, 1], x_half[1][:].indirect(entries), copy_func)
-            vcopy(x_slots[:, h, :, :, 3], x_raw[3][:].indirect(entries))
+        scopy(out=x_half[1][:, 512:], in_=x_raw[1][:, 512:])
+        vcopy(out=x_half[1][:, :512], in_=x_raw[1][:, :512])
+        sgather(1, HALF, S)
+        sgather(1, 128, HALF)
+        vgather(1, 0, 128)
+        vgather(3, HALF, S)
+        vgather(3, 0, HALF)
         quant_x(1)
         for i in range(4):
-            nc.tensor.matmul_mx(out=acc[i % 2, 1][:], lhsT=x_codes[1][:, RUN:RUN + P].bitcast(FP8X4),
-                                lhsT_scale=x_scales[1][:, RUN:RUN + P],
-                                rhs=x_codes[1][:, RUN:].bitcast(FP8X4), rhs_scale=x_scales[1][:, RUN:],
+            c0 = SPAN + RUN
+            nc.tensor.matmul_mx(out=acc[i % 2, 1][:], lhsT=x_codes[:, c0:c0 + P].bitcast(FP8X4),
+                                lhsT_scale=x_scales[:, c0:c0 + P],
+                                rhs=x_codes[:, c0:c0 + HALF].bitcast(FP8X4), rhs_scale=x_scales[:, c0:c0 + HALF],
                                 start=True, stop=True)
         quant_x(0)
+        scopy(out=front_bf[:, :, PACK:], in_=x_bf[:, :, PACK - 1, :HALF - PACK])
+        scopy(out=front_bf[:, 1, :PACK], in_=x_bf[:, 0, PACK - 1, HALF - PACK:])
+        quant_front(0)
+        quant_front(1)
         cast_w(vcopy, 0, 0, 0, P)
-        cast_w(vcopy, 0, 2, 0, 32)
-        cast_w(scopy, 0, 2, 32, P)
+        cast_w(scopy, 0, 2, 0, P)
         for t in range(PACK):
             quant_w(0, t)
             for h in range(2):
                 tap(0, h, t)
-        nc.vector.memset(prev_bf[:, 0, 0:PACK], 0.0)
-        vcopy(out=prev_bf[:, :, PACK:], in_=x_bf[:, :, PACK - 1, :HALF - PACK])
-        vcopy(out=prev_bf[:, 1, :PACK], in_=x_bf[:, 0, PACK - 1, HALF - PACK:])
-        cast_w(vcopy, 1, 0, 0, 88)
-        cast_w(scopy, 1, 0, 88, P)
-        for h in range(2):
-            nc.vector.quantize_mx(out=x_codes[h][:, :RUN].bitcast(FP8X4), scales=x_scales[h][:, :RUN],
-                                  in_=prev_bf[:, h, :])
-        cast_w(vcopy, 1, 2, 0, 56)
-        cast_w(scopy, 1, 2, 56, P)
-        for t in range(PACK):
+        cast_w2_pair(scopy, 0, 0, P)
+        cast_w2_pair(vcopy, 2, 0, 88)
+        cast_w2_pair(scopy, 2, 88, P)
+        cast_w(vcopy, 1, 2, 0, 40)
+        cast_w(scopy, 1, 2, 72, P)
+        quant_w(1, 0)
+        cast_w(vcopy, 1, 2, 40, 72)
+        for t in range(1, PACK):
             quant_w(1, t)
 
         y = sb.tile([P, PACK, S], F32, name="y", align_bytes=64)
@@ -131,18 +162,21 @@ def tile_picked_listconv_none_lo_kernel(tc, xT, w1, w2, offs, out_0, out_1, out_
                                   in_=y_bf[:, s0:s1, :].rearrange("p s t -> p (s t)"))
             nc.sync.dma_start(out=words[:, s0:s1], in_=y_codes[:, s0:s1].bitcast(I32))
 
-        for t in range(2):
-            finish(scopy, 0, t)
-            finish(vcopy, 1, t)
-            nc.sync.dma_start(out=out_rows[:, t, :], in_=y[:, t, :])
+        finish(scopy, 0, 0)
+        nc.sync.dma_start(out=out_rows[:, 0, :HALF], in_=y[:, 0, :HALF])
+        finish(vcopy, 1, 0)
+        nc.sync.dma_start(out=out_rows[:, 0, HALF:], in_=y[:, 0, HALF:])
+        finish(scopy, 0, 1)
+        finish(vcopy, 1, 1)
+        nc.sync.dma_start(out=out_rows[:, 1, :], in_=y[:, 1, :])
         finish(scopy, 0, 2)
-        finish(vcopy, 0, 3)
-        finish(scopy, 1, 2)
+        finish(scopy, 0, 3)
+        finish(vcopy, 1, 2)
         finish(scopy, 1, 3)
         nc.sync.dma_start(out=out_rows[:, 2:, :], in_=y[:, 2:, :])
         cast_y(vcopy, 0, HALF)
-        cast_y(vcopy, HALF, 384)
-        cast_y(scopy, 384, S)
+        cast_y(vcopy, HALF, 368)
+        cast_y(scopy, 368, S)
         quant_y(0, HALF)
         quant_y(HALF, S)
         for q in range(4):

@@ -134,9 +134,9 @@ def tile_picked_listconv_none_lo_kernel(tc, xT, w1, w2, offs, out_0, out_1, out_
         cast_w2_pair(vcopy, 2, 0, 88)
         cast_w2_pair(scopy, 2, 88, P)
         cast_w(vcopy, 1, 2, 0, 40)
-        cast_w(scopy, 1, 2, 72, P)
+        cast_w(scopy, 1, 2, 60, P)
         quant_w(1, 0)
-        cast_w(vcopy, 1, 2, 40, 72)
+        cast_w(vcopy, 1, 2, 40, 60)
         for t in range(1, PACK):
             quant_w(1, t)
 

@@ -30,9 +30,10 @@ def tile_picked_listconv_none_lo_kernel(tc, xT, w1, w2, offs, out_0, out_1, out_
         offsets = sb.tile([P, S // 16], U16, name="offsets")
         x_rows = xT.rearrange("(p j) t -> p j t", j=PACK)
         x_raw = [sb.tile([P, T], F32, name="x_raw%d" % j, align_bytes=64) for j in range(PACK)]
-        nc.sync.dma_start(offsets[:], offs)
         for j in (0, 2, 1, 3):
             nc.sync.dma_start(out=x_raw[j][:], in_=x_rows[:, j, :])
+            if j == 0:
+                nc.sync.dma_start(offsets[:], offs)
         w_raw = [sb.tile([P, PACK, N], F32, name="w_raw%d" % d, align_bytes=64) for d in range(2)]
         nc.sync.dma_start(out=w_raw[0][:], in_=w1.rearrange("(p j) c -> p j c", j=PACK))
         for j0 in (0, 2):

@@ -109,8 +109,7 @@ def tile_picked_listconv_none_lo_kernel(tc, xT, w1, w2, offs, out_0, out_1, out_
         scopy(out=x_half[1][:, 512:], in_=x_raw[1][:, 512:])
         vcopy(out=x_half[1][:, :512], in_=x_raw[1][:, :512])
         sgather(1, HALF, S)
-        sgather(1, 128, HALF)
-        vgather(1, 0, 128)
+        sgather(1, 0, HALF)
         vgather(3, HALF, S)
         vgather(3, 0, HALF)
         quant_x(1)

@@ -120,16 +120,19 @@ def tile_picked_listconv_none_lo_kernel(tc, xT, w1, w2, offs, out_0, out_1, out_
                                 rhs=x_codes[:, c0:c0 + HALF].bitcast(FP8X4), rhs_scale=x_scales[:, c0:c0 + HALF],
                                 start=True, stop=True)
         quant_x(0)
+        cast_w(vcopy, 0, 0, 0, 80)
+        cast_w(scopy, 0, 0, 80, P)
+        cast_w(scopy, 0, 2, 48, P)
+        for t in range(PACK):
+            quant_w(0, t)
+            if t == 0:
+                cast_w(vcopy, 0, 2, 0, 48)
+            for h in range(2):
+                tap(0, h, t)
         scopy(out=front_bf[:, :, PACK:], in_=x_bf[:, :, PACK - 1, :HALF - PACK])
         scopy(out=front_bf[:, 1, :PACK], in_=x_bf[:, 0, PACK - 1, HALF - PACK:])
         quant_front(0)
         quant_front(1)
-        cast_w(vcopy, 0, 0, 0, P)
-        cast_w(scopy, 0, 2, 0, P)
-        for t in range(PACK):
-            quant_w(0, t)
-            for h in range(2):
-                tap(0, h, t)
         cast_w2_pair(scopy, 0, 0, P)
         cast_w2_pair(vcopy, 2, 0, 88)
         cast_w2_pair(scopy, 2, 88, P)

@@ -122,11 +122,11 @@ def tile_picked_listconv_none_lo_kernel(tc, xT, w1, w2, offs, out_0, out_1, out_
         quant_x(0)
         cast_w(vcopy, 0, 0, 0, 80)
         cast_w(scopy, 0, 0, 80, P)
-        cast_w(scopy, 0, 2, 48, P)
+        cast_w(scopy, 0, 2, 68, P)
         for t in range(PACK):
             quant_w(0, t)
             if t == 0:
-                cast_w(vcopy, 0, 2, 0, 48)
+                cast_w(vcopy, 0, 2, 0, 68)
             for h in range(2):
                 tap(0, h, t)
         scopy(out=front_bf[:, :, PACK:], in_=x_bf[:, :, PACK - 1, :HALF - PACK])

@@ -18,6 +18,7 @@ PACK = 4
 HALF = 256
 RUN = HALF // PACK
 SPAN = RUN + HALF
+LEAD = 32
 
 
 def tile_picked_listconv_none_lo_kernel(tc, xT, w1, w2, offs, out_0, out_1, out_2):
@@ -42,10 +43,13 @@ def tile_picked_listconv_none_lo_kernel(tc, xT, w1, w2, offs, out_0, out_1, out_
 
         x_half = [sb.tile([P, T], BF16, name="x_half%d" % j, align_bytes=64) for j in range(2)]
         x_bf = sb.tile([P, 2, PACK, RUN * PACK], BF16, name="x_bf", align_bytes=64)
-        front_bf = sb.tile([P, 2, RUN * PACK], BF16, name="front_bf", align_bytes=64)
         x_codes = sb.tile([P, 2 * SPAN], U32, name="x_codes", align_bytes=64)
         x_scales = sb.tile([P, 2 * SPAN], U8, name="x_scales", align_bytes=64)
-        w_bf = [sb.tile([P, PACK, P, PACK], BF16, name="w_bf%d" % d, align_bytes=64) for d in range(2)]
+        w_tiles = [[sb.tile([P, LEAD + 2 * P * PACK], BF16, name="w_bf%d%d" % (d, u), align_bytes=64)
+                    for u in range(2)] for d in range(2)]
+        w_bf = [[w_tiles[d][u][:, LEAD:].rearrange("p (t m j) -> p t m j", t=2, j=PACK) for u in range(2)]
+                for d in range(2)]
+        front_bf = w_tiles[0][0][:, :2 * RUN * PACK]
         w_codes = [sb.tile([P, N], U32, name="w_codes%d" % d, align_bytes=64) for d in range(2)]
         w_scales = [sb.tile([P, N], U8, name="w_scales%d" % d, align_bytes=64) for d in range(2)]
 
@@ -70,23 +74,23 @@ def tile_picked_listconv_none_lo_kernel(tc, xT, w1, w2, offs, out_0, out_1, out_
         def quant_front(h):
             c0 = h * SPAN
             nc.vector.quantize_mx(out=x_codes[:, c0:c0 + RUN].bitcast(FP8X4), scales=x_scales[:, c0:c0 + RUN],
-                                  in_=front_bf[:, h, :])
+                                  in_=front_bf[:, h * RUN * PACK:(h + 1) * RUN * PACK])
 
         def cast_w(copy, d, t0, m0, m1):
             src = w_raw[d][:].rearrange("p j (m t) -> p m j t", t=PACK)
-            copy(out=w_bf[d][:, t0:t0 + 2, m0:m1, :].rearrange("p t m j -> p m j t"),
+            copy(out=w_bf[d][t0 // 2][:, :, m0:m1, :].rearrange("p t m j -> p m j t"),
                  in_=src[:, m0:m1, :, t0:t0 + 2])
 
         def cast_w2_pair(copy, j0, m0, m1):
             src = w_raw[1][:, j0:j0 + 2, :].rearrange("p j (a i t) -> p a t i j", i=2, t=PACK)
-            dst = w_bf[1][:, :, :, j0:j0 + 2].rearrange("p t (a i) j -> p a t i j", i=2)
-            copy(out=dst[:, m0 // 2:m1 // 2, 0:2], in_=src[:, m0 // 2:m1 // 2, 0:2])
+            dst = w_bf[1][0][:, :, :, j0:j0 + 2].rearrange("p t (a i) j -> p a t i j", i=2)
+            copy(out=dst[:, m0 // 2:m1 // 2], in_=src[:, m0 // 2:m1 // 2, 0:2])
 
         def quant_w(d, t):
             nc.vector.quantize_mx(
                 out=w_codes[d][:, t * P:(t + 1) * P].bitcast(FP8X4),
                 scales=w_scales[d][:, t * P:(t + 1) * P],
-                in_=w_bf[d][:, t, :, :].rearrange("p m j -> p (m j)"))
+                in_=w_bf[d][t // 2][:, t % 2, :, :].rearrange("p m j -> p (m j)"))
 
         acc = {(h, t): psum.tile([P, HALF], F32, name="acc%d%d" % (h, t)) for h in range(2) for t in range(PACK)}
 
@@ -100,7 +104,7 @@ def tile_picked_listconv_none_lo_kernel(tc, xT, w1, w2, offs, out_0, out_1, out_
 
         zeros = sb.tile([P, PACK], BF16, name="zeros")
         nc.vector.memset(zeros[:], 0.0)
-        nc.scalar.activation(front_bf[:, 0, :PACK], zeros[:], copy_func)
+        nc.scalar.activation(front_bf[:, :PACK], zeros[:], copy_func)
         vcopy(out=x_half[0][:], in_=x_raw[0][:])
         sgather(0, HALF, S)
         sgather(0, 128, HALF)
@@ -113,24 +117,21 @@ def tile_picked_listconv_none_lo_kernel(tc, xT, w1, w2, offs, out_0, out_1, out_
         vgather(3, HALF, S)
         vgather(3, 0, HALF)
         quant_x(1)
-        for i in range(4):
-            c0 = SPAN + RUN
-            nc.tensor.matmul_mx(out=acc[i % 2, 1][:], lhsT=x_codes[:, c0:c0 + P].bitcast(FP8X4),
-                                lhsT_scale=x_scales[:, c0:c0 + P],
-                                rhs=x_codes[:, c0:c0 + HALF].bitcast(FP8X4), rhs_scale=x_scales[:, c0:c0 + HALF],
-                                start=True, stop=True)
         quant_x(0)
-        cast_w(vcopy, 0, 0, 0, 80)
-        cast_w(scopy, 0, 0, 80, P)
-        cast_w(scopy, 0, 2, 68, P)
+        nc.tensor.matmul_mx(out=acc[1, 3][:], lhsT=x_codes[:, RUN:RUN + P].bitcast(FP8X4), lhsT_scale=x_scales[:, RUN:RUN + P],
+                            rhs=x_codes[:, RUN:SPAN].bitcast(FP8X4), rhs_scale=x_scales[:, RUN:SPAN],
+                            start=True, stop=True)
+        cast_w(vcopy, 0, 0, 0, 72)
+        cast_w(scopy, 0, 0, 72, P)
+        cast_w(scopy, 0, 2, 48, P)
         for t in range(PACK):
             quant_w(0, t)
             if t == 0:
-                cast_w(vcopy, 0, 2, 0, 68)
+                cast_w(vcopy, 0, 2, 0, 48)
             for h in range(2):
                 tap(0, h, t)
-        scopy(out=front_bf[:, :, PACK:], in_=x_bf[:, :, PACK - 1, :HALF - PACK])
-        scopy(out=front_bf[:, 1, :PACK], in_=x_bf[:, 0, PACK - 1, HALF - PACK:])
+        vcopy(out=front_bf.rearrange("p (h n) -> p h n", h=2)[:, :, PACK:], in_=x_bf[:, :, PACK - 1, :HALF - PACK])
+        vcopy(out=front_bf[:, HALF:HALF + PACK], in_=x_bf[:, 0, PACK - 1, HALF - PACK:])
         quant_front(0)
         quant_front(1)
         cast_w2_pair(scopy, 0, 0, P)

@@ -66,15 +66,19 @@ def tile_picked_listconv_none_lo_kernel(tc, xT, w1, w2, offs, out_0, out_1, out_
         def sgather(j, s0, s1):
             nc.scalar.activation(slots(j, s0, s1), x_half[j][:].indirect(offsets[:, s0 // 16:s1 // 16]), copy_func)
 
+        def quant_cols(c0, src):
+            n = src.shape[1] // PACK
+            nc.vector.quantize_mx(out=x_codes[:, c0:c0 + n].bitcast(FP8X4), scales=x_scales[:, c0:c0 + n], in_=src)
+
         def quant_x(h):
-            c0 = h * SPAN + RUN
-            nc.vector.quantize_mx(out=x_codes[:, c0:c0 + HALF].bitcast(FP8X4), scales=x_scales[:, c0:c0 + HALF],
-                                  in_=x_bf[:, h, :, :].rearrange("p r n -> p (r n)"))
+            if h == 1:
+                quant_cols(RUN, x_bf[:, 1, :, :].rearrange("p r n -> p (r n)"))
+            else:
+                for r in range(PACK):
+                    quant_cols(SPAN + (PACK - 1 - r) * RUN, x_bf[:, 0, r, :])
 
         def quant_front(h):
-            c0 = h * SPAN
-            nc.vector.quantize_mx(out=x_codes[:, c0:c0 + RUN].bitcast(FP8X4), scales=x_scales[:, c0:c0 + RUN],
-                                  in_=front_bf[:, h * RUN * PACK:(h + 1) * RUN * PACK])
+            quant_cols(0 if h == 1 else SPAN + HALF, front_bf[:, h * RUN * PACK:(h + 1) * RUN * PACK])
 
         def cast_w(copy, d, t0, m0, m1):
             src = w_raw[d][:].rearrange("p j (m t) -> p m j t", t=PACK)
@@ -92,11 +96,12 @@ def tile_picked_listconv_none_lo_kernel(tc, xT, w1, w2, offs, out_0, out_1, out_
                 scales=w_scales[d][:, t * P:(t + 1) * P],
                 in_=w_bf[d][t // 2][:, t % 2, :, :].rearrange("p m j -> p (m j)"))
 
-        acc = {(h, t): psum.tile([P, HALF], F32, name="acc%d%d" % (h, t)) for h in range(2) for t in range(PACK)}
+        banks = {(h, t): psum.tile([P, S], F32, name="acc%d%d" % (h, t)) for h in range(2) for t in range(PACK)}
+        acc = {key: bank[:, :HALF] for key, bank in banks.items()}
 
         def tap(d, h, t):
-            c0 = h * SPAN + RUN * (1 - d)
-            nc.tensor.matmul_mx(out=acc[h, t][:], lhsT=w_codes[d][:, t * P:(t + 1) * P].bitcast(FP8X4),
+            c0 = RUN * (1 - d) if h == 1 else SPAN + RUN * d
+            nc.tensor.matmul_mx(out=acc[h, t], lhsT=w_codes[d][:, t * P:(t + 1) * P].bitcast(FP8X4),
                                 lhsT_scale=w_scales[d][:, t * P:(t + 1) * P],
                                 rhs=x_codes[:, c0:c0 + HALF].bitcast(FP8X4),
                                 rhs_scale=x_scales[:, c0:c0 + HALF],
@@ -118,8 +123,8 @@ def tile_picked_listconv_none_lo_kernel(tc, xT, w1, w2, offs, out_0, out_1, out_
         vgather(3, 0, HALF)
         quant_x(1)
         quant_x(0)
-        nc.tensor.matmul_mx(out=acc[1, 3][:], lhsT=x_codes[:, RUN:RUN + P].bitcast(FP8X4), lhsT_scale=x_scales[:, RUN:RUN + P],
-                            rhs=x_codes[:, RUN:SPAN].bitcast(FP8X4), rhs_scale=x_scales[:, RUN:SPAN],
+        nc.tensor.matmul_mx(out=banks[1, 3][:], lhsT=x_codes[:, RUN:RUN + P].bitcast(FP8X4), lhsT_scale=x_scales[:, RUN:RUN + P],
+                            rhs=x_codes[:, RUN:RUN + S].bitcast(FP8X4), rhs_scale=x_scales[:, RUN:RUN + S],
                             start=True, stop=True)
         cast_w(vcopy, 0, 0, 0, 72)
         cast_w(scopy, 0, 0, 72, P)
@@ -154,8 +159,9 @@ def tile_picked_listconv_none_lo_kernel(tc, xT, w1, w2, offs, out_0, out_1, out_
 
         def finish(copy, h, t):
             tap(1, h, t)
+            runs = acc[h, t].rearrange("p (r c) -> p c r", r=PACK)
             copy(out=y[:, t, h * HALF:(h + 1) * HALF].rearrange("p (c r) -> p c r", r=PACK),
-                 in_=acc[h, t][:].rearrange("p (r c) -> p c r", r=PACK))
+                 in_=runs if h == 1 else runs[:, :, ::-1])
 
         def cast_y(copy, s0, s1):
             copy(out=y_bf[:, s0:s1, :].rearrange("p (c i) t -> p c t i", i=PACK),

@@ -37,9 +37,7 @@ def tile_picked_listconv_none_lo_kernel(tc, xT, w1, w2, offs, out_0, out_1, out_
                 nc.sync.dma_start(offsets[:], offs)
         w_raw = [sb.tile([P, PACK, N], F32, name="w_raw%d" % d, align_bytes=64) for d in range(2)]
         nc.sync.dma_start(out=w_raw[0][:], in_=w1.rearrange("(p j) c -> p j c", j=PACK))
-        for j0 in (0, 2):
-            nc.sync.dma_start(out=w_raw[1][:, j0:j0 + 2, :],
-                              in_=w2.rearrange("(p j) c -> p j c", j=PACK)[:, j0:j0 + 2, :])
+        nc.sync.dma_start(out=w_raw[1][:], in_=w2.rearrange("(p j) c -> p j c", j=PACK))
 
         x_half = [sb.tile([P, T], BF16, name="x_half%d" % j, align_bytes=64) for j in range(2)]
         x_bf = sb.tile([P, 2, PACK, RUN * PACK], BF16, name="x_bf", align_bytes=64)
@@ -66,29 +64,20 @@ def tile_picked_listconv_none_lo_kernel(tc, xT, w1, w2, offs, out_0, out_1, out_
         def sgather(j, s0, s1):
             nc.scalar.activation(slots(j, s0, s1), x_half[j][:].indirect(offsets[:, s0 // 16:s1 // 16]), copy_func)
 
-        def quant_cols(c0, src):
-            n = src.shape[1] // PACK
-            nc.vector.quantize_mx(out=x_codes[:, c0:c0 + n].bitcast(FP8X4), scales=x_scales[:, c0:c0 + n], in_=src)
-
         def quant_x(h):
-            if h == 1:
-                quant_cols(RUN, x_bf[:, 1, :, :].rearrange("p r n -> p (r n)"))
-            else:
-                for r in range(PACK):
-                    quant_cols(SPAN + (PACK - 1 - r) * RUN, x_bf[:, 0, r, :])
+            c0 = h * SPAN + RUN
+            nc.vector.quantize_mx(out=x_codes[:, c0:c0 + HALF].bitcast(FP8X4), scales=x_scales[:, c0:c0 + HALF],
+                                  in_=x_bf[:, h, :, :].rearrange("p r n -> p (r n)"))
 
         def quant_front(h):
-            quant_cols(0 if h == 1 else SPAN + HALF, front_bf[:, h * RUN * PACK:(h + 1) * RUN * PACK])
+            c0 = h * SPAN
+            nc.vector.quantize_mx(out=x_codes[:, c0:c0 + RUN].bitcast(FP8X4), scales=x_scales[:, c0:c0 + RUN],
+                                  in_=front_bf[:, h * RUN * PACK:(h + 1) * RUN * PACK])
 
         def cast_w(copy, d, t0, m0, m1):
             src = w_raw[d][:].rearrange("p j (m t) -> p m j t", t=PACK)
             copy(out=w_bf[d][t0 // 2][:, :, m0:m1, :].rearrange("p t m j -> p m j t"),
                  in_=src[:, m0:m1, :, t0:t0 + 2])
-
-        def cast_w2_pair(copy, j0, m0, m1):
-            src = w_raw[1][:, j0:j0 + 2, :].rearrange("p j (a i t) -> p a t i j", i=2, t=PACK)
-            dst = w_bf[1][0][:, :, :, j0:j0 + 2].rearrange("p t (a i) j -> p a t i j", i=2)
-            copy(out=dst[:, m0 // 2:m1 // 2], in_=src[:, m0 // 2:m1 // 2, 0:2])
 
         def quant_w(d, t):
             nc.vector.quantize_mx(
@@ -96,12 +85,11 @@ def tile_picked_listconv_none_lo_kernel(tc, xT, w1, w2, offs, out_0, out_1, out_
                 scales=w_scales[d][:, t * P:(t + 1) * P],
                 in_=w_bf[d][t // 2][:, t % 2, :, :].rearrange("p m j -> p (m j)"))
 
-        banks = {(h, t): psum.tile([P, S], F32, name="acc%d%d" % (h, t)) for h in range(2) for t in range(PACK)}
-        acc = {key: bank[:, :HALF] for key, bank in banks.items()}
+        acc = {(h, t): psum.tile([P, HALF], F32, name="acc%d%d" % (h, t)) for h in range(2) for t in range(PACK)}
 
         def tap(d, h, t):
-            c0 = RUN * (1 - d) if h == 1 else SPAN + RUN * d
-            nc.tensor.matmul_mx(out=acc[h, t], lhsT=w_codes[d][:, t * P:(t + 1) * P].bitcast(FP8X4),
+            c0 = h * SPAN + RUN * (1 - d)
+            nc.tensor.matmul_mx(out=acc[h, t][:], lhsT=w_codes[d][:, t * P:(t + 1) * P].bitcast(FP8X4),
                                 lhsT_scale=w_scales[d][:, t * P:(t + 1) * P],
                                 rhs=x_codes[:, c0:c0 + HALF].bitcast(FP8X4),
                                 rhs_scale=x_scales[:, c0:c0 + HALF],
@@ -123,29 +111,27 @@ def tile_picked_listconv_none_lo_kernel(tc, xT, w1, w2, offs, out_0, out_1, out_
         vgather(3, 0, HALF)
         quant_x(1)
         quant_x(0)
-        nc.tensor.matmul_mx(out=banks[1, 3][:], lhsT=x_codes[:, RUN:RUN + P].bitcast(FP8X4), lhsT_scale=x_scales[:, RUN:RUN + P],
-                            rhs=x_codes[:, RUN:RUN + S].bitcast(FP8X4), rhs_scale=x_scales[:, RUN:RUN + S],
+        nc.tensor.matmul_mx(out=acc[1, 3][:], lhsT=x_codes[:, RUN:RUN + P].bitcast(FP8X4), lhsT_scale=x_scales[:, RUN:RUN + P],
+                            rhs=x_codes[:, RUN:SPAN].bitcast(FP8X4), rhs_scale=x_scales[:, RUN:SPAN],
                             start=True, stop=True)
-        cast_w(vcopy, 0, 0, 0, 72)
-        cast_w(scopy, 0, 0, 72, P)
-        cast_w(scopy, 0, 2, 48, P)
+        cast_w(vcopy, 0, 0, 0, 76)
+        cast_w(scopy, 0, 0, 76, P)
+        cast_w(vcopy, 0, 2, 0, 24)
+        cast_w(scopy, 0, 2, 24, P)
         for t in range(PACK):
             quant_w(0, t)
-            if t == 0:
-                cast_w(vcopy, 0, 2, 0, 48)
             for h in range(2):
                 tap(0, h, t)
         vcopy(out=front_bf.rearrange("p (h n) -> p h n", h=2)[:, :, PACK:], in_=x_bf[:, :, PACK - 1, :HALF - PACK])
         vcopy(out=front_bf[:, HALF:HALF + PACK], in_=x_bf[:, 0, PACK - 1, HALF - PACK:])
         quant_front(0)
         quant_front(1)
-        cast_w2_pair(scopy, 0, 0, P)
-        cast_w2_pair(vcopy, 2, 0, 88)
-        cast_w2_pair(scopy, 2, 88, P)
-        cast_w(vcopy, 1, 2, 0, 40)
-        cast_w(scopy, 1, 2, 60, P)
+        cast_w(vcopy, 1, 0, 0, 80)
+        cast_w(scopy, 1, 0, 80, P)
+        cast_w(vcopy, 1, 2, 0, 32)
+        cast_w(scopy, 1, 2, 68, P)
         quant_w(1, 0)
-        cast_w(vcopy, 1, 2, 40, 60)
+        cast_w(vcopy, 1, 2, 32, 68)
         for t in range(1, PACK):
             quant_w(1, t)
 
@@ -159,9 +145,8 @@ def tile_picked_listconv_none_lo_kernel(tc, xT, w1, w2, offs, out_0, out_1, out_
 
         def finish(copy, h, t):
             tap(1, h, t)
-            runs = acc[h, t].rearrange("p (r c) -> p c r", r=PACK)
             copy(out=y[:, t, h * HALF:(h + 1) * HALF].rearrange("p (c r) -> p c r", r=PACK),
-                 in_=runs if h == 1 else runs[:, :, ::-1])
+                 in_=acc[h, t][:].rearrange("p (r c) -> p c r", r=PACK))
 
         def cast_y(copy, s0, s1):
             copy(out=y_bf[:, s0:s1, :].rearrange("p (c i) t -> p c t i", i=PACK),
@@ -175,10 +160,10 @@ def tile_picked_listconv_none_lo_kernel(tc, xT, w1, w2, offs, out_0, out_1, out_
         finish(scopy, 0, 0)
         nc.sync.dma_start(out=out_rows[:, 0, :HALF], in_=y[:, 0, :HALF])
         finish(vcopy, 1, 0)
-        nc.sync.dma_start(out=out_rows[:, 0, HALF:], in_=y[:, 0, HALF:])
         finish(scopy, 0, 1)
         finish(vcopy, 1, 1)
-        nc.sync.dma_start(out=out_rows[:, 1, :], in_=y[:, 1, :])
+        nc.sync.dma_start(out=out_rows.rearrange("p t s -> p (t s)")[:, HALF:2 * S],
+                          in_=y[:].rearrange("p t s -> p (t s)")[:, HALF:2 * S])
         finish(scopy, 0, 2)
         finish(scopy, 0, 3)
         finish(vcopy, 1, 2)

@@ -111,9 +111,6 @@ def tile_picked_listconv_none_lo_kernel(tc, xT, w1, w2, offs, out_0, out_1, out_
         vgather(3, 0, HALF)
         quant_x(1)
         quant_x(0)
-        nc.tensor.matmul_mx(out=acc[1, 3][:], lhsT=x_codes[:, RUN:RUN + P].bitcast(FP8X4), lhsT_scale=x_scales[:, RUN:RUN + P],
-                            rhs=x_codes[:, RUN:SPAN].bitcast(FP8X4), rhs_scale=x_scales[:, RUN:SPAN],
-                            start=True, stop=True)
         cast_w(vcopy, 0, 0, 0, 76)
         cast_w(scopy, 0, 0, 76, P)
         cast_w(vcopy, 0, 2, 0, 24)

@@ -123,12 +123,12 @@ def tile_picked_listconv_none_lo_kernel(tc, xT, w1, w2, offs, out_0, out_1, out_
         vcopy(out=front_bf[:, HALF:HALF + PACK], in_=x_bf[:, 0, PACK - 1, HALF - PACK:])
         quant_front(0)
         quant_front(1)
-        cast_w(vcopy, 1, 0, 0, 80)
-        cast_w(scopy, 1, 0, 80, P)
-        cast_w(vcopy, 1, 2, 0, 32)
-        cast_w(scopy, 1, 2, 68, P)
+        cast_w(vcopy, 1, 0, 0, 84)
+        cast_w(scopy, 1, 0, 84, P)
+        cast_w(vcopy, 1, 2, 0, 56)
+        cast_w(scopy, 1, 2, 80, P)
         quant_w(1, 0)
-        cast_w(vcopy, 1, 2, 32, 68)
+        cast_w(vcopy, 1, 2, 56, 80)
         for t in range(1, PACK):
             quant_w(1, t)
 
@@ -154,21 +154,18 @@ def tile_picked_listconv_none_lo_kernel(tc, xT, w1, w2, offs, out_0, out_1, out_
                                   in_=y_bf[:, s0:s1, :].rearrange("p s t -> p (s t)"))
             nc.sync.dma_start(out=words[:, s0:s1], in_=y_codes[:, s0:s1].bitcast(I32))
 
-        finish(scopy, 0, 0)
-        nc.sync.dma_start(out=out_rows[:, 0, :HALF], in_=y[:, 0, :HALF])
-        finish(vcopy, 1, 0)
-        finish(scopy, 0, 1)
-        finish(vcopy, 1, 1)
-        nc.sync.dma_start(out=out_rows.rearrange("p t s -> p (t s)")[:, HALF:2 * S],
-                          in_=y[:].rearrange("p t s -> p (t s)")[:, HALF:2 * S])
-        finish(scopy, 0, 2)
-        finish(scopy, 0, 3)
-        finish(vcopy, 1, 2)
-        finish(scopy, 1, 3)
+        for t in range(PACK):
+            finish(scopy, 0, t)
+            if t == 0:
+                nc.sync.dma_start(out=out_rows[:, 0, :HALF], in_=y[:, 0, :HALF])
+            finish(vcopy, 1, t)
+            if t == 1:
+                nc.sync.dma_start(out=out_rows.rearrange("p t s -> p (t s)")[:, HALF:2 * S],
+                                  in_=y[:].rearrange("p t s -> p (t s)")[:, HALF:2 * S])
         nc.sync.dma_start(out=out_rows[:, 2:, :], in_=y[:, 2:, :])
-        cast_y(vcopy, 0, HALF)
-        cast_y(vcopy, HALF, 368)
-        cast_y(scopy, 368, S)
+        for h in range(2):
+            cast_y(vcopy, h * HALF, h * HALF + 168)
+            cast_y(scopy, h * HALF + 168, (h + 1) * HALF)
         quant_y(0, HALF)
         quant_y(HALF, S)
         for q in range(4):

from contextlib import ExitStack

import concourse.mybir as mybir

K, T, S, N = 512, 1024, 512, 512
FLOPS = 2 * 2 * K * N * S

F32 = mybir.dt.float32
BF16 = mybir.dt.bfloat16
U32 = mybir.dt.uint32
I32 = mybir.dt.int32
U16 = mybir.dt.uint16
U8 = mybir.dt.uint8
FP8X4 = mybir.dt.float8_e4m3fn_x4

P = 128
PACK = 4
HALF = 256
RUN = HALF // PACK
SPAN = RUN + HALF
LEAD = 32


def tile_picked_listconv_none_lo_kernel(tc, xT, w1, w2, offs, out_0, out_1, out_2):
    nc = tc.nc
    vcopy, scopy = nc.vector.tensor_copy, nc.scalar.copy
    with ExitStack() as ctx:
        sb = ctx.enter_context(tc.tile_pool(name="sb", bufs=1))
        psum = ctx.enter_context(tc.psum_pool(name="psum", bufs=1))

        offsets = sb.tile([P, S // 16], U16, name="offsets")
        x_rows = xT.rearrange("(p j) t -> p j t", j=PACK)
        x_raw = [sb.tile([P, T], F32, name="x_raw%d" % j, align_bytes=64) for j in range(PACK)]
        for j in (0, 2, 1, 3):
            nc.sync.dma_start(out=x_raw[j][:], in_=x_rows[:, j, :])
            if j == 0:
                nc.sync.dma_start(offsets[:], offs)
        w_raw = [sb.tile([P, PACK, N], F32, name="w_raw%d" % d, align_bytes=64) for d in range(2)]
        nc.sync.dma_start(out=w_raw[0][:], in_=w1.rearrange("(p j) c -> p j c", j=PACK))
        nc.sync.dma_start(out=w_raw[1][:], in_=w2.rearrange("(p j) c -> p j c", j=PACK))

        x_half = [sb.tile([P, T], BF16, name="x_half%d" % j, align_bytes=64) for j in range(2)]
        x_bf = sb.tile([P, 2, PACK, RUN * PACK], BF16, name="x_bf", align_bytes=64)
        x_codes = sb.tile([P, 2 * SPAN], U32, name="x_codes", align_bytes=64)
        x_scales = sb.tile([P, 2 * SPAN], U8, name="x_scales", align_bytes=64)
        w_tiles = [[sb.tile([P, LEAD + 2 * P * PACK], BF16, name="w_bf%d%d" % (d, u), align_bytes=64)
                    for u in range(2)] for d in range(2)]
        w_bf = [[w_tiles[d][u][:, LEAD:].rearrange("p (t m j) -> p t m j", t=2, j=PACK) for u in range(2)]
                for d in range(2)]
        front_bf = w_tiles[0][0][:, :2 * RUN * PACK]
        w_codes = [sb.tile([P, N], U32, name="w_codes%d" % d, align_bytes=64) for d in range(2)]
        w_scales = [sb.tile([P, N], U8, name="w_scales%d" % d, align_bytes=64) for d in range(2)]

        copy_func = mybir.ActivationFunctionType.Copy
        x_slots = x_bf[:].rearrange("p h r (c j) -> p h c r j", j=PACK)

        def slots(j, s0, s1):
            h, c0 = divmod(s0 // PACK, RUN)
            return x_slots[:, h, c0:c0 + (s1 - s0) // PACK, :, j]

        def vgather(j, s0, s1):
            vcopy(slots(j, s0, s1), x_raw[j][:].indirect(offsets[:, s0 // 16:s1 // 16]))

        def sgather(j, s0, s1):
            nc.scalar.activation(slots(j, s0, s1), x_half[j][:].indirect(offsets[:, s0 // 16:s1 // 16]), copy_func)

        def quant_x(h):
            c0 = h * SPAN + RUN
            nc.vector.quantize_mx(out=x_codes[:, c0:c0 + HALF].bitcast(FP8X4), scales=x_scales[:, c0:c0 + HALF],
                                  in_=x_bf[:, h, :, :].rearrange("p r n -> p (r n)"))

        def quant_front(h):
            c0 = h * SPAN
            nc.vector.quantize_mx(out=x_codes[:, c0:c0 + RUN].bitcast(FP8X4), scales=x_scales[:, c0:c0 + RUN],
                                  in_=front_bf[:, h * RUN * PACK:(h + 1) * RUN * PACK])

        def cast_w(copy, d, t0, m0, m1):
            src = w_raw[d][:].rearrange("p j (m t) -> p m j t", t=PACK)
            copy(out=w_bf[d][t0 // 2][:, :, m0:m1, :].rearrange("p t m j -> p m j t"),
                 in_=src[:, m0:m1, :, t0:t0 + 2])

        def quant_w(d, t):
            nc.vector.quantize_mx(
                out=w_codes[d][:, t * P:(t + 1) * P].bitcast(FP8X4),
                scales=w_scales[d][:, t * P:(t + 1) * P],
                in_=w_bf[d][t // 2][:, t % 2, :, :].rearrange("p m j -> p (m j)"))

        acc = {(h, t): psum.tile([P, HALF], F32, name="acc%d%d" % (h, t)) for h in range(2) for t in range(PACK)}

        def tap(d, h, t):
            c0 = h * SPAN + RUN * (1 - d)
            nc.tensor.matmul_mx(out=acc[h, t][:], lhsT=w_codes[d][:, t * P:(t + 1) * P].bitcast(FP8X4),
                                lhsT_scale=w_scales[d][:, t * P:(t + 1) * P],
                                rhs=x_codes[:, c0:c0 + HALF].bitcast(FP8X4),
                                rhs_scale=x_scales[:, c0:c0 + HALF],
                                start=(d == 0), stop=(d == 1))

        zeros = sb.tile([P, PACK], BF16, name="zeros")
        nc.vector.memset(zeros[:], 0.0)
        nc.scalar.activation(front_bf[:, :PACK], zeros[:], copy_func)
        vcopy(out=x_half[0][:], in_=x_raw[0][:])
        sgather(0, HALF, S)
        sgather(0, 128, HALF)
        vgather(0, 0, 128)
        vcopy(x_slots[:, :, :, :, 2], x_raw[2][:].indirect(offsets[:]))
        scopy(out=x_half[1][:, 512:], in_=x_raw[1][:, 512:])
        vcopy(out=x_half[1][:, :512], in_=x_raw[1][:, :512])
        sgather(1, HALF, S)
        sgather(1, 0, HALF)
        vgather(3, HALF, S)
        vgather(3, 0, HALF)
        quant_x(1)
        quant_x(0)
        cast_w(vcopy, 0, 0, 0, 76)
        cast_w(scopy, 0, 0, 76, P)
        cast_w(vcopy, 0, 2, 0, 24)
        cast_w(scopy, 0, 2, 24, P)
        for t in range(PACK):
            quant_w(0, t)
            for h in range(2):
                tap(0, h, t)
        vcopy(out=front_bf.rearrange("p (h n) -> p h n", h=2)[:, :, PACK:], in_=x_bf[:, :, PACK - 1, :HALF - PACK])
        vcopy(out=front_bf[:, HALF:HALF + PACK], in_=x_bf[:, 0, PACK - 1, HALF - PACK:])
        quant_front(0)
        quant_front(1)
        cast_w(vcopy, 1, 0, 0, 84)
        cast_w(scopy, 1, 0, 84, P)
        cast_w(vcopy, 1, 2, 0, 56)
        cast_w(scopy, 1, 2, 80, P)
        quant_w(1, 0)
        cast_w(vcopy, 1, 2, 56, 80)
        for t in range(1, PACK):
            quant_w(1, t)

        y = sb.tile([P, PACK, S], F32, name="y", align_bytes=64)
        y_bf = sb.tile([P, S, PACK], BF16, name="y_bf", align_bytes=64)
        y_codes = sb.tile([P, S], U32, name="y_codes", align_bytes=64)
        y_scales = sb.tile([P, S], U8, name="y_scales", align_bytes=64)
        out_rows = out_0.rearrange("(p t) s -> p t s", t=PACK)
        words = out_1.rearrange("z l c r -> l (z c r)").bitcast(I32)
        scale_rows = out_2.rearrange("z q c -> (z q) c").bitcast(I32)

        def finish(copy, h, t):
            tap(1, h, t)
            copy(out=y[:, t, h * HALF:(h + 1) * HALF].rearrange("p (c r) -> p c r", r=PACK),
                 in_=acc[h, t][:].rearrange("p (r c) -> p c r", r=PACK))

        def cast_y(copy, s0, s1):
            copy(out=y_bf[:, s0:s1, :].rearrange("p (c i) t -> p c t i", i=PACK),
                 in_=y[:, :, s0:s1].rearrange("p t (c i) -> p c t i", i=PACK))

        def quant_y(s0, s1):
            nc.vector.quantize_mx(out=y_codes[:, s0:s1].bitcast(FP8X4), scales=y_scales[:, s0:s1],
                                  in_=y_bf[:, s0:s1, :].rearrange("p s t -> p (s t)"))
            nc.sync.dma_start(out=words[:, s0:s1], in_=y_codes[:, s0:s1].bitcast(I32))

        for t in range(PACK):
            finish(scopy, 0, t)
            if t == 0:
                nc.sync.dma_start(out=out_rows[:, 0, :HALF], in_=y[:, 0, :HALF])
            finish(vcopy, 1, t)
            if t == 1:
                nc.sync.dma_start(out=out_rows.rearrange("p t s -> p (t s)")[:, HALF:2 * S],
                                  in_=y[:].rearrange("p t s -> p (t s)")[:, HALF:2 * S])
        nc.sync.dma_start(out=out_rows[:, 2:, :], in_=y[:, 2:, :])
        for h in range(2):
            cast_y(vcopy, h * HALF, h * HALF + 168)
            cast_y(scopy, h * HALF + 168, (h + 1) * HALF)
        quant_y(0, HALF)
        quant_y(HALF, S)
        for q in range(4):
            queue = nc.scalar if q % 2 == 0 else nc.sync
            queue.dma_start(out=scale_rows[4 * q:4 * q + 4, :], in_=y_scales[32 * q:32 * q + 4, :].bitcast(I32))
